import numpy as np
import ml_dtypes


def mxq(x, axis, fmt="e4m3"):
    dtype, down = {"e4m3": (ml_dtypes.float8_e4m3fn, 7), "e5m2": (ml_dtypes.float8_e5m2, 14)}[fmt]
    v = np.moveaxis(np.asarray(x, np.float32).astype(ml_dtypes.bfloat16).astype(np.float64), axis, -1)
    blocks = v.reshape(v.shape[:-1] + (-1, 32))
    amax = np.abs(blocks).max(-1, keepdims=True)
    byte = np.maximum(np.where(amax > 0, np.frexp(amax)[1] - 1 + 127, 0) - down, 1)
    scale = np.exp2(byte - 127.0)
    codes = (blocks / scale).astype(np.float32).astype(dtype).astype(np.float64)
    return np.moveaxis((codes * scale).reshape(v.shape), -1, axis)


WIDE = False


def mx_kscale(k):
    if not WIDE:
        return np.ones(k)
    levels = np.array([10, -10, 5, -5, 0])
    if k % 512:
        return np.exp2(np.random.permutation(np.resize(levels, k // 32))).repeat(32)
    a = np.empty((k // 512, 16))
    for p in range(k // 512):
        a[p, :8] = np.random.permutation(np.resize(levels, 8))
        for g in range(8):
            far = levels[np.abs(levels - a[p, g]) >= 10]
            a[p, g + 8] = far[np.random.randint(len(far))]
    return np.exp2(a.ravel()).repeat(32)


def f64(x):
    return np.asarray(x).astype(np.float64)


def striped(idx):
    return np.tile(idx.reshape(-1, 16).T, (8, 1)).astype(np.uint16)


def unstriped(offs):
    return offs[:16].T.reshape(-1).astype(np.int64)


E2M1 = np.array([0.0, 0.5, 1.0, 1.5, 2.0, 3.0, 4.0, 6.0, -0.0, -0.5, -1.0, -1.5, -2.0, -3.0, -4.0, -6.0])


def pack_weight(w, fmt):
    k, n = w.shape
    w = f64(np.asarray(w, np.float32).astype(ml_dtypes.bfloat16)).reshape(k // 32, 32, n)
    amax = np.abs(w).max(1)
    if fmt == "e4m3":
        byte = np.frexp(amax)[1] - 1 + 127 - 7
    else:
        mant, ex = np.frexp(amax / 6.0)
        byte = np.where(mant > 0.5, ex, ex - 1) + 127
    byte = np.clip(np.where(amax > 0, byte, 1), 1, 254)
    scaled = (w * np.exp2(127.0 - byte)[:, None, :]).reshape(k, n).astype(np.float32)
    by_word = np.ascontiguousarray(scaled.reshape(k // 512, 128, 4, n).transpose(0, 1, 3, 2))
    if fmt == "e4m3":
        words = by_word.astype(ml_dtypes.float8_e4m3fn).view(np.uint8)
    else:
        c = by_word.astype(ml_dtypes.float4_e2m1fn).view(np.uint8) & 0xF
        words = (c[..., 0::2] | (c[..., 1::2] << 4)).reshape(k // 512, 128, 2 * n)
    return np.ascontiguousarray(words), np.ascontiguousarray(byte.astype(np.uint8).reshape(k // 512, 16, n))


def unpack_weight(words, scales, fmt):
    g, _, n = scales.shape
    words = np.ascontiguousarray(words).reshape(g, 128, n, -1)
    if fmt == "e4m3":
        vals = words.view(ml_dtypes.float8_e4m3fn).astype(np.float64)
    else:
        nib = np.empty((g, 128, n, 4), np.uint8)
        nib[..., 0::2] = words & 0xF
        nib[..., 1::2] = words >> 4
        vals = E2M1[nib]
    vals = vals * np.repeat(np.exp2(scales.astype(np.float64) - 127.0), 8, axis=1)[..., None]
    return vals.transpose(0, 1, 3, 2).reshape(g * 512, n)


def relu2(v):
    return np.maximum(v, 0.0) ** 2


K, T, E, C, H, N = 512, 1280, 10, 256, 512, 128


def by_expert(wq, xq):
    return np.concatenate([wq[e].T @ xq[:, e * C:(e + 1) * C] for e in range(E)], axis=1)


def setup_inputs():
    n = np.random.standard_normal
    s = mx_kscale(K)[:, None]
    u = mx_kscale(H)
    first = np.random.permutation(np.repeat(np.arange(E), T // E))
    second = (first + 1 + np.random.permutation(np.repeat(np.arange(E - 1), -(-T // (E - 1)))[:T])) % E
    while np.bincount(second, minlength=E).max() != T // E:
        load = np.bincount(second, minlength=E); hi, lo = int(load.argmax()), int(load.argmin())
        t = np.flatnonzero((second == hi) & (first != lo))[0]; second[t] = lo
    slot_token = np.empty(E * C, np.int64); pos = np.empty((2, T), np.int64); fill = np.zeros(E, np.int64)
    place = np.stack([np.random.permutation(C) for _ in range(E)])
    for r, deal in enumerate((first, second)):
        for t in np.random.permutation(T):
            e = deal[t]; j = e * C + place[e, fill[e]]; fill[e] += 1; slot_token[j] = t; pos[r, t] = j
    g = np.random.uniform(0.2, 0.8, T)
    w1 = [pack_weight(m, "e2m1") for m in n((E, K, H)) / np.sqrt(K) / s[None] * u[None, None, :]]
    w2 = [pack_weight(m, "e2m1") for m in n((E, H, N)) / np.sqrt(H) / u[None, :, None] ** 2]
    w_slot = np.empty(E * C); w_slot[pos[0]] = g; w_slot[pos[1]] = 1.0 - g
    return {
        "xT": (n((K, T)) * s).astype(np.float32),
        "w1_words": np.stack([m[0] for m in w1]),
        "w1_scales": np.stack([m[1] for m in w1]),
        "w2_words": np.stack([m[0] for m in w2]),
        "w2_scales": np.stack([m[1] for m in w2]),
        "gate": np.tile(w_slot, (K, 1)).astype(np.float32),
        "offs": striped(slot_token),
        "pos1": striped(pos[0]),
        "pos2": striped(pos[1]),
    }


def reference(xT, w1_words, w1_scales, w2_words, w2_scales, gate, offs, pos1, pos2):
    idx = unstriped(offs)
    w1 = np.stack([unpack_weight(w1_words[e], w1_scales[e], "e2m1") for e in range(E)])
    w2 = np.stack([unpack_weight(w2_words[e], w2_scales[e], "e2m1") for e in range(E)])
    xq = mxq(f64(gate) * f64(xT)[:, idx], 0, "e4m3")
    h = relu2(by_expert(w1, xq))
    y = by_expert(w2, mxq(h, 0, "e4m3"))
    return y[:, unstriped(pos1)] + y[:, unstriped(pos2)]

@@ -1,0 +1,227 @@
+from contextlib import ExitStack
+
+import concourse.mybir as mybir
+from concourse.masks import make_identity
+
+K, T, E, C, H, N = 512, 1280, 10, 256, 512, 128
+S = E * C
+FLOPS = 2 * S * (K * H + H * N)
+
+F32 = mybir.dt.float32
+BF16 = mybir.dt.bfloat16
+I32 = mybir.dt.int32
+U32 = mybir.dt.uint32
+U16 = mybir.dt.uint16
+U8 = mybir.dt.uint8
+FP8X4 = mybir.dt.float8_e4m3fn_x4
+FP4X4 = mybir.dt.float4_e2m1fn_x4
+ALU = mybir.AluOpType
+ACT = mybir.ActivationFunctionType
+
+P = 128
+PACK = 4
+AHEAD = 2
+VECTOR_SLOTS = 128
+GATE_CUTS = (0, 2, 5, 10)
+W1_CUTS = (0, 2, 6, 10)
+S1_CUTS = (0, 2, 10)
+OUT_CUTS = (0, 448, 896, 1152, 1280)
+
+
+def tile_moe_pre_mlp_relu2_kernel(
+    tc, xT, w1_words, w1_scales, w2_words, w2_scales, gate, offs, pos1, pos2, out
+):
+    nc = tc.nc
+    with ExitStack() as ctx:
+        lists = ctx.enter_context(tc.tile_pool(name="lists", bufs=1))
+        keep = ctx.enter_context(tc.tile_pool(name="keep", bufs=1))
+        chain = ctx.enter_context(tc.tile_pool(name="chain", bufs=1))
+        ring = ctx.enter_context(tc.tile_pool(name="ring", bufs=3))
+        psum_a = ctx.enter_context(tc.psum_pool(name="psum_a", bufs=3))
+        psum_t = ctx.enter_context(tc.psum_pool(name="psum_t", bufs=3))
+        psum_y = ctx.enter_context(tc.psum_pool(name="psum_y", bufs=2))
+
+        offs_sb = lists.tile([P, S // 16], U16, name="offs_sb")
+        pos1_sb = lists.tile([P, T // 16], U16, name="pos1_sb")
+        pos2_sb = lists.tile([P, T // 16], U16, name="pos2_sb")
+
+        def pieces(cuts, width, dtype, label):
+            tiles = []
+            where = {}
+            for j in range(len(cuts) - 1):
+                tile = keep.tile([P, (cuts[j + 1] - cuts[j]) * width], dtype, name=label + str(j), align_bytes=64)
+                tiles.append(tile)
+                for e in range(cuts[j], cuts[j + 1]):
+                    where[e] = tile[:, (e - cuts[j]) * width : (e - cuts[j] + 1) * width]
+            return tiles, where
+
+        x_sb = [keep.tile([P, T], F32, name="x" + str(t), align_bytes=64) for t in range(PACK)]
+        gate_tiles, gate_of = pieces(GATE_CUTS, C, F32, "gate")
+        w1_tiles, w1_of = pieces(W1_CUTS, 2 * H, U8, "w1")
+        s1_tiles, s1_of = pieces(S1_CUTS, H, U8, "s1")
+        w2_tiles, w2_of = pieces((0, E), 2 * N, U8, "w2")
+        s2_tiles, s2_of = pieces((0, E), N, U8, "s2")
+        y_sb = keep.tile([P, S], F32, name="y_sb", align_bytes=64)
+
+        nc.gpsimd.memset(s1_tiles[0][:].bitcast(I32), 0)
+        for plane in s2_tiles + s1_tiles[1:]:
+            nc.vector.memset(plane[:].bitcast(I32), 0)
+
+        made = keep.tile([P, P], F32, name="made")
+        ident = keep.tile([P, P], F32, name="ident")
+        make_identity(nc, made[:])
+        nc.scalar.activation(ident[:], made[:], ACT.Relu)
+
+        x_rows = xT.rearrange("(p t) w -> p t w", t=PACK)
+
+        def load_gate(j):
+            nc.sync.dma_start(gate_tiles[j][:], gate[0:P, GATE_CUTS[j] * C : GATE_CUTS[j + 1] * C])
+
+        def load_words(tile, words, e0, e1):
+            nc.sync.dma_start(
+                tile[:].bitcast(I32).rearrange("p (e n) -> p e n", e=e1 - e0),
+                words.rearrange("e s p n -> p (e s) n")[:, e0:e1, :].bitcast(I32),
+            )
+
+        def load_scales(tile, scales, e0, e1):
+            rows = scales.rearrange("e s (q r) n -> r q (e s) n", r=4)
+            for r in range(4):
+                nc.sync.dma_start(
+                    tile[r:P:32, :].bitcast(I32).rearrange("p (e n) -> p e n", e=e1 - e0),
+                    rows[r][:, e0:e1, :].bitcast(I32),
+                )
+
+        nc.sync.dma_start(offs_sb[:], offs)
+        nc.sync.dma_start(x_sb[0][:], x_rows[:, 0, :])
+        load_gate(0)
+        for t in range(1, PACK):
+            nc.sync.dma_start(x_sb[t][:], x_rows[:, t, :])
+        load_words(w1_tiles[0], w1_words, W1_CUTS[0], W1_CUTS[1])
+        load_scales(s1_tiles[0], w1_scales, S1_CUTS[0], S1_CUTS[1])
+        load_gate(1)
+        load_words(w2_tiles[0], w2_words, 0, E)
+        load_scales(s2_tiles[0], w2_scales, 0, E)
+        load_words(w1_tiles[1], w1_words, W1_CUTS[1], W1_CUTS[2])
+        load_scales(s1_tiles[1], w1_scales, S1_CUTS[1], S1_CUTS[2])
+        load_gate(2)
+        load_words(w1_tiles[2], w1_words, W1_CUTS[2], W1_CUTS[3])
+        nc.sync.dma_start(pos1_sb[:], pos1)
+        nc.sync.dma_start(pos2_sb[:], pos2)
+
+        gated, x_bf, x_q, relu, turned, h_bf, h_q, acc = {}, {}, {}, {}, {}, {}, {}, {}
+
+        def link(shape, dtype, tag):
+            return chain.tile(shape, dtype, name="link", tag=tag, align_bytes=64)
+
+        def gather(e, t):
+            if t == 0:
+                gated[e] = link([P, PACK, C], F32, "K" + str(e - 3) if e >= AHEAD else "G" + str(e))
+            nc.vector.tensor_tensor(
+                gated[e][:, t, :],
+                x_sb[t][:].indirect(offs_sb[:, e * (C // 16) : (e + 1) * (C // 16)]),
+                gate_of[e],
+                ALU.mult,
+            )
+
+        def weave(e):
+            x_bf[e] = link([P, C * PACK], BF16, "K" + str(e - 1))
+            cut = C if e == E - 1 else VECTOR_SLOTS
+            dst = x_bf[e][:, : cut * PACK].rearrange("p (c i t) -> p c t i", i=2, t=PACK)
+            nc.vector.tensor_copy(dst, gated[e][:, :, :cut].rearrange("p t (c i) -> p c t i", i=2))
+            if cut < C:
+                dst = x_bf[e][:, cut * PACK :].rearrange("p (c i t) -> p c t i", i=2, t=PACK)
+                nc.scalar.copy(dst, gated[e][:, :, cut:].rearrange("p t (c i) -> p c t i", i=2))
+
+        def quantise(values, tag, label):
+            codes = link([P, C], U32, tag)
+            scales = ring.tile([P, C], U8, name=label, align_bytes=64)
+            nc.vector.quantize_mx(out=codes[:].bitcast(FP8X4), scales=scales[:], in_=values[:])
+            return codes, scales
+
+        def first_layer(e):
+            codes, scales = x_q[e]
+            pre = {}
+            for half in range(2):
+                cols = slice(half * P, (half + 1) * P)
+                pre[half] = psum_a.tile([P, H], F32, name="pre")
+                nc.tensor.matmul_mx(
+                    out=pre[half][:],
+                    lhsT=codes[:, cols].bitcast(FP8X4),
+                    lhsT_scale=scales[:, cols],
+                    rhs=w1_of[e].bitcast(FP4X4),
+                    rhs_scale=s1_of[e],
+                    start=True,
+                    stop=True,
+                )
+            for half in range(2):
+                if half == 0:
+                    relu[half] = link([P, PACK, P], F32, "R" + str(e))
+                else:
+                    relu[half] = ring.tile([P, PACK, P], F32, name="relu_b", align_bytes=64)
+                src = pre[half][:].rearrange("p (m t) -> p t m", t=PACK)
+                if e == E - 1 and half == 1:
+                    nc.vector.tensor_scalar_max(relu[half][:], src, 0.0)
+                else:
+                    nc.scalar.activation(relu[half][:], src, ACT.Relu)
+            for half in range(2):
+                turned[e, half] = psum_t.tile([P, PACK, P], F32, name="turned")
+                for t in range(PACK):
+                    nc.tensor.transpose(turned[e, half][:, t, :], relu[half][:, t, :], ident[:])
+
+        def square(e):
+            h_bf[e] = link([P, C * PACK], BF16, "K" + str(e + 2))
+            for half in range(2):
+                nc.scalar.activation(
+                    h_bf[e][:, half * P * PACK : (half + 1) * P * PACK].rearrange("p (s t) -> p s t", t=PACK),
+                    turned[e, half][:].rearrange("p t s -> p s t"),
+                    ACT.Square,
+                )
+
+        def second_layer(e):
+            codes, scales = quantise(h_bf[e], "R" + str(e + 1), "h_scales")
+            acc[e] = psum_y.tile([P, C], F32, name="acc")
+            nc.tensor.matmul_mx(
+                out=acc[e][:],
+                lhsT=w2_of[e].bitcast(FP4X4),
+                lhsT_scale=s2_of[e],
+                rhs=codes[:].bitcast(FP8X4),
+                rhs_scale=scales[:],
+                start=True,
+                stop=True,
+            )
+
+        for t in range(PACK - 1):
+            for e in range(AHEAD):
+                gather(e, t)
+        gather(0, PACK - 1)
+        weave(0)
+        gather(1, PACK - 1)
+        for e in range(E + 2):
+            if e < E:
+                x_q[e] = quantise(x_bf[e], "K" + str(e), "x_scales")
+            if e + AHEAD < E:
+                for t in range(PACK):
+                    gather(e + AHEAD, t)
+            if 1 <= e <= E:
+                square(e - 1)
+            if e >= 2:
+                nc.scalar.copy(y_sb[:, (e - 2) * C : (e - 1) * C], acc[e - 2][:])
+            if e < E:
+                first_layer(e)
+            if e + 1 < E:
+                weave(e + 1)
+            if 1 <= e <= E:
+                second_layer(e - 1)
+
+        first = keep.tile([P, T], F32, name="first", align_bytes=64)
+        for half in range(2):
+            c0, c1 = half * T // 2, (half + 1) * T // 2
+            nc.vector.tensor_copy(first[:, c0:c1], y_sb[:].indirect(pos1_sb[:, c0 // 16 : c1 // 16]))
+        for j in range(len(OUT_CUTS) - 1):
+            c0, c1 = OUT_CUTS[j], OUT_CUTS[j + 1]
+            total = keep.tile([P, c1 - c0], F32, name="total" + str(j), align_bytes=64)
+            nc.vector.tensor_tensor(
+                total[:], y_sb[:].indirect(pos2_sb[:, c0 // 16 : c1 // 16]), first[:, c0:c1], ALU.add
+            )
+            queue = nc.sync if j % 2 == 0 else nc.scalar
+            queue.dma_start(out[:, c0:c1], total[:])

@@ -21,7 +21,7 @@ ACT = mybir.ActivationFunctionType
 P = 128
 PACK = 4
 AHEAD = 2
-VECTOR_SLOTS = 128
+LAST = E - 1
 GATE_CUTS = (0, 2, 5, 10)
 W1_CUTS = (0, 2, 6, 10)
 S1_CUTS = (0, 2, 10)
@@ -37,9 +37,7 @@ def tile_moe_pre_mlp_relu2_kernel(
         keep = ctx.enter_context(tc.tile_pool(name="keep", bufs=1))
         chain = ctx.enter_context(tc.tile_pool(name="chain", bufs=1))
         ring = ctx.enter_context(tc.tile_pool(name="ring", bufs=3))
-        psum_a = ctx.enter_context(tc.psum_pool(name="psum_a", bufs=3))
-        psum_t = ctx.enter_context(tc.psum_pool(name="psum_t", bufs=3))
-        psum_y = ctx.enter_context(tc.psum_pool(name="psum_y", bufs=2))
+        psum = ctx.enter_context(tc.psum_pool(name="psum", bufs=1))
 
         offs_sb = lists.tile([P, S // 16], U16, name="offs_sb")
         pos1_sb = lists.tile([P, T // 16], U16, name="pos1_sb")
@@ -108,10 +106,13 @@ def tile_moe_pre_mlp_relu2_kernel(
         nc.sync.dma_start(pos1_sb[:], pos1)
         nc.sync.dma_start(pos2_sb[:], pos2)
 
-        gated, x_bf, x_q, relu, turned, h_bf, h_q, acc = {}, {}, {}, {}, {}, {}, {}, {}
+        gated, x_bf, x_q, turned, h_bf, h_q, acc = {}, {}, {}, {}, {}, {}, {}
 
         def link(shape, dtype, tag):
             return chain.tile(shape, dtype, name="link", tag=tag, align_bytes=64)
+
+        def bank(shape, tag):
+            return psum.tile(shape, F32, name="bank", tag=tag)
 
         def gather(e, t):
             if t == 0:
@@ -123,27 +124,41 @@ def tile_moe_pre_mlp_relu2_kernel(
                 ALU.mult,
             )
 
-        def weave(e):
-            x_bf[e] = link([P, C * PACK], BF16, "K" + str(e - 1))
-            cut = C if e == E - 1 else VECTOR_SLOTS
-            dst = x_bf[e][:, : cut * PACK].rearrange("p (c i t) -> p c t i", i=2, t=PACK)
-            nc.vector.tensor_copy(dst, gated[e][:, :, :cut].rearrange("p t (c i) -> p c t i", i=2))
-            if cut < C:
-                dst = x_bf[e][:, cut * PACK :].rearrange("p (c i t) -> p c t i", i=2, t=PACK)
-                nc.scalar.copy(dst, gated[e][:, :, cut:].rearrange("p t (c i) -> p c t i", i=2))
+        def weave(e, half):
+            if half == 0:
+                tile = link([P, P * PACK], BF16, "K" + str(min(e, LAST - 1) - 1))
+            elif e >= LAST - 1:
+                tile = link([P, P * PACK], BF16, "M")
+            else:
+                tile = ring.tile([P, P * PACK], BF16, name="x_half", align_bytes=64)
+            x_bf[e, half] = tile
+            dst = tile[:].rearrange("p (c i t) -> p c t i", i=4, t=PACK)
+            src = gated[e][:, :, half * P : (half + 1) * P].rearrange("p t (c i) -> p c t i", i=4)
+            if half == 0 or e == LAST:
+                nc.vector.tensor_copy(dst, src)
+            else:
+                nc.scalar.copy(dst, src)
 
-        def quantise(values, tag, label):
-            codes = link([P, C], U32, tag)
-            scales = ring.tile([P, C], U8, name=label, align_bytes=64)
-            nc.vector.quantize_mx(out=codes[:].bitcast(FP8X4), scales=scales[:], in_=values[:])
-            return codes, scales
-
-        def first_layer(e):
-            codes, scales = x_q[e]
-            pre = {}
+        def quantise_x(e):
+            codes = link([P, C], U32, "K" + str(e) if e < LAST else "L")
+            scales = ring.tile([P, C], U8, name="x_scales", align_bytes=64)
             for half in range(2):
                 cols = slice(half * P, (half + 1) * P)
-                pre[half] = psum_a.tile([P, H], F32, name="pre")
+                nc.vector.quantize_mx(out=codes[:, cols].bitcast(FP8X4), scales=scales[:, cols], in_=x_bf[e, half][:])
+            x_q[e] = codes, scales
+
+        def quantise_h(e):
+            codes = ring.tile([P, C], U32, name="h_codes", align_bytes=64)
+            scales = ring.tile([P, C], U8, name="h_scales", align_bytes=64)
+            nc.vector.quantize_mx(out=codes[:].bitcast(FP8X4), scales=scales[:], in_=h_bf[e][:])
+            h_q[e] = codes, scales
+
+        def first_product(e):
+            codes, scales = x_q[e]
+            pre = []
+            for half in range(2):
+                cols = slice(half * P, (half + 1) * P)
+                pre.append(bank([P, H], "X" + str((e + half) % 2) if e < LAST else "Z" + str(half)))
                 nc.tensor.matmul_mx(
                     out=pre[half][:],
                     lhsT=codes[:, cols].bitcast(FP8X4),
@@ -153,18 +168,23 @@ def tile_moe_pre_mlp_relu2_kernel(
                     start=True,
                     stop=True,
                 )
+            return pre
+
+        def relu_and_turn(e, pre):
+            relu = []
             for half in range(2):
-                if half == 0:
-                    relu[half] = link([P, PACK, P], F32, "R" + str(e))
+                if e == LAST - 2 and half == 1:
+                    relu.append(link([P, PACK, P], F32, "L"))
                 else:
-                    relu[half] = ring.tile([P, PACK, P], F32, name="relu_b", align_bytes=64)
-                src = pre[half][:].rearrange("p (m t) -> p t m", t=PACK)
-                if e == E - 1 and half == 1:
-                    nc.vector.tensor_scalar_max(relu[half][:], src, 0.0)
+                    relu.append(ring.tile([P, PACK, P], F32, name="relu", align_bytes=64, bufs=4))
+                dst = relu[half][:].rearrange("p t (c i) -> p c t i", i=2)
+                src = pre[half][:].rearrange("p (c i t) -> p c t i", i=2, t=PACK)
+                if 2 * e + half >= 2 * E - 3:
+                    nc.vector.tensor_scalar_max(dst, src, 0.0)
                 else:
-                    nc.scalar.activation(relu[half][:], src, ACT.Relu)
+                    nc.scalar.activation(dst, src, ACT.Relu)
             for half in range(2):
-                turned[e, half] = psum_t.tile([P, PACK, P], F32, name="turned")
+                turned[e, half] = bank([P, PACK, P], "XY"[half] + str(e % 2) if e < LAST else "Z" + str(half))
                 for t in range(PACK):
                     nc.tensor.transpose(turned[e, half][:, t, :], relu[half][:, t, :], ident[:])
 
@@ -177,9 +197,9 @@ def tile_moe_pre_mlp_relu2_kernel(
                     ACT.Square,
                 )
 
-        def second_layer(e):
-            codes, scales = quantise(h_bf[e], "R" + str(e + 1), "h_scales")
-            acc[e] = psum_y.tile([P, C], F32, name="acc")
+        def second_product(e):
+            codes, scales = h_q[e]
+            acc[e] = bank([P, C], "Y" + str((e + 1) % 2) if e < LAST - 1 else "W" + str(e % 2))
             nc.tensor.matmul_mx(
                 out=acc[e][:],
                 lhsT=w2_of[e].bitcast(FP4X4),
@@ -194,24 +214,32 @@ def tile_moe_pre_mlp_relu2_kernel(
             for e in range(AHEAD):
                 gather(e, t)
         gather(0, PACK - 1)
-        weave(0)
+        weave(0, 0)
+        weave(0, 1)
         gather(1, PACK - 1)
+        weave(1, 1)
         for e in range(E + 2):
             if e < E:
-                x_q[e] = quantise(x_bf[e], "K" + str(e), "x_scales")
+                quantise_x(e)
             if e + AHEAD < E:
                 for t in range(PACK):
                     gather(e + AHEAD, t)
+            if e < E:
+                pre = first_product(e)
+            if e + 1 < E:
+                weave(e + 1, 0)
             if 1 <= e <= E:
-                square(e - 1)
+                quantise_h(e - 1)
+            if e < E:
+                relu_and_turn(e, pre)
+            if e + 2 < E:
+                weave(e + 2, 1)
             if e >= 2:
                 nc.scalar.copy(y_sb[:, (e - 2) * C : (e - 1) * C], acc[e - 2][:])
             if e < E:
-                first_layer(e)
-            if e + 1 < E:
-                weave(e + 1)
+                square(e)
             if 1 <= e <= E:
-                second_layer(e - 1)
+                second_product(e - 1)
 
         first = keep.tile([P, T], F32, name="first", align_bytes=64)
         for half in range(2):

@@ -20,9 +20,10 @@ ACT = mybir.ActivationFunctionType
 
 P = 128
 PACK = 4
-AHEAD = 2
+PAIRS = E // 2
+G = 2 * C
 LAST = E - 1
-GATE_CUTS = (0, 2, 5, 10)
+GATE_CUTS = (0, 1, 2, 5)
 W1_CUTS = (0, 2, 6, 10)
 S1_CUTS = (0, 2, 10)
 OUT_CUTS = (0, 448, 896, 1152, 1280)
@@ -54,7 +55,7 @@ def tile_moe_pre_mlp_relu2_kernel(
             return tiles, where
 
         x_sb = [keep.tile([P, T], F32, name="x" + str(t), align_bytes=64) for t in range(PACK)]
-        gate_tiles, gate_of = pieces(GATE_CUTS, C, F32, "gate")
+        gate_tiles, gate_of = pieces(GATE_CUTS, G, F32, "gate")
         w1_tiles, w1_of = pieces(W1_CUTS, 2 * H, U8, "w1")
         s1_tiles, s1_of = pieces(S1_CUTS, H, U8, "s1")
         w2_tiles, w2_of = pieces((0, E), 2 * N, U8, "w2")
@@ -73,7 +74,7 @@ def tile_moe_pre_mlp_relu2_kernel(
         x_rows = xT.rearrange("(p t) w -> p t w", t=PACK)
 
         def load_gate(j):
-            nc.sync.dma_start(gate_tiles[j][:], gate[0:P, GATE_CUTS[j] * C : GATE_CUTS[j + 1] * C])
+            nc.sync.dma_start(gate_tiles[j][:], gate[0:P, GATE_CUTS[j] * G : GATE_CUTS[j + 1] * G])
 
         def load_words(tile, words, e0, e1):
             nc.sync.dma_start(
@@ -106,45 +107,44 @@ def tile_moe_pre_mlp_relu2_kernel(
         nc.sync.dma_start(pos1_sb[:], pos1)
         nc.sync.dma_start(pos2_sb[:], pos2)
 
-        gated, x_bf, x_q, turned, h_bf, h_q, acc = {}, {}, {}, {}, {}, {}, {}
+        gated, x_bf, x_q, pre, turned, h_bf, h_q, acc = {}, {}, {}, {}, {}, {}, {}, {}
 
         def link(shape, dtype, tag):
             return chain.tile(shape, dtype, name="link", tag=tag, align_bytes=64)
 
-        def bank(shape, tag):
-            return psum.tile(shape, F32, name="bank", tag=tag)
+        def bank(shape, e, half):
+            return psum.tile(shape, F32, name="bank", tag="bank" + str(e % 2) + str(half))
 
-        def gather(e, t):
+        def gather(k, t):
+            if k == PAIRS:
+                return
             if t == 0:
-                gated[e] = link([P, PACK, C], F32, "K" + str(e - 3) if e >= AHEAD else "G" + str(e))
+                gated[k] = link([P, PACK, G], F32, "even" + str(k - 1))
             nc.vector.tensor_tensor(
-                gated[e][:, t, :],
-                x_sb[t][:].indirect(offs_sb[:, e * (C // 16) : (e + 1) * (C // 16)]),
-                gate_of[e],
+                gated[k][:, t, :],
+                x_sb[t][:].indirect(offs_sb[:, k * (G // 16) : (k + 1) * (G // 16)]),
+                gate_of[k],
                 ALU.mult,
             )
 
-        def weave(e, half):
-            if half == 0:
-                tile = link([P, P * PACK], BF16, "K" + str(min(e, LAST - 1) - 1))
-            elif e >= LAST - 1:
-                tile = link([P, P * PACK], BF16, "M")
-            else:
-                tile = ring.tile([P, P * PACK], BF16, name="x_half", align_bytes=64)
-            x_bf[e, half] = tile
-            dst = tile[:].rearrange("p (c i t) -> p c t i", i=4, t=PACK)
-            src = gated[e][:, :, half * P : (half + 1) * P].rearrange("p t (c i) -> p c t i", i=4)
-            if half == 0 or e == LAST:
-                nc.vector.tensor_copy(dst, src)
-            else:
-                nc.scalar.copy(dst, src)
+        def weave(e):
+            k, odd = divmod(e, 2)
+            x_bf[e] = link([P, C * PACK], BF16, ("odd" if odd else "even") + str(k))
+            for c0, c1 in [(0, C)] if odd else [(0, P), (P, C)]:
+                dst = x_bf[e][:, c0 * PACK : c1 * PACK].rearrange("p (c i t) -> p c t i", i=4, t=PACK)
+                src = gated[k][:, :, odd * C + c0 : odd * C + c1].rearrange("p t (c i) -> p c t i", i=4)
+                if odd:
+                    nc.scalar.copy(dst, src)
+                else:
+                    nc.vector.tensor_copy(dst, src)
 
         def quantise_x(e):
-            codes = link([P, C], U32, "K" + str(e) if e < LAST else "L")
-            scales = ring.tile([P, C], U8, name="x_scales", align_bytes=64)
-            for half in range(2):
-                cols = slice(half * P, (half + 1) * P)
-                nc.vector.quantize_mx(out=codes[:, cols].bitcast(FP8X4), scales=scales[:, cols], in_=x_bf[e, half][:])
+            codes = ring.tile([P, C], U32, name="x_codes", align_bytes=64, bufs=4)
+            scales = ring.tile([P, C], U8, name="x_scales", align_bytes=64, bufs=4)
+            for c0, c1 in [(0, C)] if e % 2 else [(0, P), (P, C)]:
+                nc.vector.quantize_mx(
+                    out=codes[:, c0:c1].bitcast(FP8X4), scales=scales[:, c0:c1], in_=x_bf[e][:, c0 * PACK : c1 * PACK]
+                )
             x_q[e] = codes, scales
 
         def quantise_h(e):
@@ -155,12 +155,11 @@ def tile_moe_pre_mlp_relu2_kernel(
 
         def first_product(e):
             codes, scales = x_q[e]
-            pre = []
             for half in range(2):
                 cols = slice(half * P, (half + 1) * P)
-                pre.append(bank([P, H], "X" + str((e + half) % 2) if e < LAST else "Z" + str(half)))
+                pre[e, half] = bank([P, H], e, half)
                 nc.tensor.matmul_mx(
-                    out=pre[half][:],
+                    out=pre[e, half][:],
                     lhsT=codes[:, cols].bitcast(FP8X4),
                     lhsT_scale=scales[:, cols],
                     rhs=w1_of[e].bitcast(FP4X4),
@@ -168,38 +167,42 @@ def tile_moe_pre_mlp_relu2_kernel(
                     start=True,
                     stop=True,
                 )
-            return pre
 
-        def relu_and_turn(e, pre):
+        def relu_and_turn(e):
             relu = []
             for half in range(2):
-                if e == LAST - 2 and half == 1:
-                    relu.append(link([P, PACK, P], F32, "L"))
+                if e % 2 and half:
+                    relu.append(link([P, PACK, P], F32, "odd" + str(e // 2 + 1)))
                 else:
-                    relu.append(ring.tile([P, PACK, P], F32, name="relu", align_bytes=64, bufs=4))
+                    relu.append(ring.tile([P, PACK, P], F32, name="relu", align_bytes=64))
                 dst = relu[half][:].rearrange("p t (c i) -> p c t i", i=2)
-                src = pre[half][:].rearrange("p (c i t) -> p c t i", i=2, t=PACK)
-                if 2 * e + half >= 2 * E - 3:
+                src = pre[e, half][:].rearrange("p (c i t) -> p c t i", i=2, t=PACK)
+                if e >= E - 2 and half:
                     nc.vector.tensor_scalar_max(dst, src, 0.0)
                 else:
                     nc.scalar.activation(dst, src, ACT.Relu)
             for half in range(2):
-                turned[e, half] = bank([P, PACK, P], "XY"[half] + str(e % 2) if e < LAST else "Z" + str(half))
+                turned[e, half] = bank([P, PACK, P], e, half)
                 for t in range(PACK):
                     nc.tensor.transpose(turned[e, half][:, t, :], relu[half][:, t, :], ident[:])
 
-        def square(e):
-            h_bf[e] = link([P, C * PACK], BF16, "K" + str(e + 2))
-            for half in range(2):
-                nc.scalar.activation(
-                    h_bf[e][:, half * P * PACK : (half + 1) * P * PACK].rearrange("p (s t) -> p s t", t=PACK),
-                    turned[e, half][:].rearrange("p t s -> p s t"),
-                    ACT.Square,
-                )
+        def square(e, half):
+            if half == 0 and e % 2:
+                h_bf[e] = ring.tile([P, C * PACK], BF16, name="h_odd", align_bytes=64)
+            elif half == 0:
+                h_bf[e] = link([P, C * PACK], BF16, "even" + str(e // 2 + 1))
+            nc.scalar.activation(
+                h_bf[e][:, half * P * PACK : (half + 1) * P * PACK].rearrange("p (s t) -> p s t", t=PACK),
+                turned[e, half][:].rearrange("p t s -> p s t"),
+                ACT.Square,
+            )
 
         def second_product(e):
             codes, scales = h_q[e]
-            acc[e] = bank([P, C], "Y" + str((e + 1) % 2) if e < LAST - 1 else "W" + str(e % 2))
+            if e % 2 and e < LAST:
+                acc[e] = bank([P, C], e + 1, 0)
+            else:
+                acc[e] = psum.tile([P, C], F32, name="acc", bufs=2)
             nc.tensor.matmul_mx(
                 out=acc[e][:],
                 lhsT=w2_of[e].bitcast(FP4X4),
@@ -210,36 +213,50 @@ def tile_moe_pre_mlp_relu2_kernel(
                 stop=True,
             )
 
-        for t in range(PACK - 1):
-            for e in range(AHEAD):
-                gather(e, t)
-        gather(0, PACK - 1)
-        weave(0, 0)
-        weave(0, 1)
-        gather(1, PACK - 1)
-        weave(1, 1)
-        for e in range(E + 2):
-            if e < E:
-                quantise_x(e)
-            if e + AHEAD < E:
-                for t in range(PACK):
-                    gather(e + AHEAD, t)
-            if e < E:
-                pre = first_product(e)
-            if e + 1 < E:
-                weave(e + 1, 0)
-            if 1 <= e <= E:
-                quantise_h(e - 1)
-            if e < E:
-                relu_and_turn(e, pre)
-            if e + 2 < E:
-                weave(e + 2, 1)
-            if e >= 2:
-                nc.scalar.copy(y_sb[:, (e - 2) * C : (e - 1) * C], acc[e - 2][:])
-            if e < E:
-                square(e)
-            if 1 <= e <= E:
-                second_product(e - 1)
+        def keep_result(e):
+            if e in (E - 4, E - 3):
+                nc.vector.tensor_copy(y_sb[:, e * C : (e + 1) * C], acc[e][:])
+            else:
+                nc.scalar.copy(y_sb[:, e * C : (e + 1) * C], acc[e][:])
+
+        for t in range(PACK):
+            gather(0, t)
+        for k in range(PAIRS):
+            a, b = 2 * k, 2 * k + 1
+            if k:
+                quantise_h(a - 2)
+                second_product(a - 2)
+            weave(a)
+            weave(b)
+            if k:
+                square(b - 2, 0)
+                square(b - 2, 1)
+            quantise_x(a)
+            quantise_x(b)
+            first_product(a)
+            first_product(b)
+            gather(k + 1, 0)
+            if k:
+                quantise_h(b - 2)
+                keep_result(a - 2)
+            for t in range(1, PACK):
+                gather(k + 1, t)
+            relu_and_turn(a)
+            relu_and_turn(b)
+            square(a, 0)
+            if k:
+                second_product(b - 2)
+            square(a, 1)
+            if k:
+                keep_result(b - 2)
+        square(LAST, 0)
+        quantise_h(LAST - 1)
+        square(LAST, 1)
+        second_product(LAST - 1)
+        quantise_h(LAST)
+        keep_result(LAST - 1)
+        second_product(LAST)
+        keep_result(LAST)
 
         first = keep.tile([P, T], F32, name="first", align_bytes=64)
         for half in range(2):

@@ -26,7 +26,8 @@ LAST = E - 1
 GATE_CUTS = (0, 1, 2, 5)
 W1_CUTS = (0, 2, 6, 10)
 S1_CUTS = (0, 2, 10)
-OUT_CUTS = (0, 448, 896, 1152, 1280)
+OUT_CUTS = (0, 640, 1088, 1280)
+ROOM = 9216
 
 
 def tile_moe_pre_mlp_relu2_kernel(
@@ -37,6 +38,7 @@ def tile_moe_pre_mlp_relu2_kernel(
         lists = ctx.enter_context(tc.tile_pool(name="lists", bufs=1))
         keep = ctx.enter_context(tc.tile_pool(name="keep", bufs=1))
         chain = ctx.enter_context(tc.tile_pool(name="chain", bufs=1))
+        arena = ctx.enter_context(tc.tile_pool(name="arena", bufs=1))
         ring = ctx.enter_context(tc.tile_pool(name="ring", bufs=3))
         psum = ctx.enter_context(tc.psum_pool(name="psum", bufs=1))
 
@@ -112,6 +114,9 @@ def tile_moe_pre_mlp_relu2_kernel(
         def link(shape, dtype, tag):
             return chain.tile(shape, dtype, name="link", tag=tag, align_bytes=64)
 
+        def placed(shape, dtype, name, k, start):
+            return arena.tile(shape, dtype, name=name + str(k), align_bytes=64, offset=k * ROOM + start)
+
         def bank(shape, e, half):
             return psum.tile(shape, F32, name="bank", tag="bank" + str(e % 2) + str(half))
 
@@ -119,7 +124,7 @@ def tile_moe_pre_mlp_relu2_kernel(
             if k == PAIRS:
                 return
             if t == 0:
-                gated[k] = link([P, PACK, G], F32, "even" + str(k - 1))
+                gated[k] = placed([P, PACK, G], F32, "gated", k, 0)
             nc.vector.tensor_tensor(
                 gated[k][:, t, :],
                 x_sb[t][:].indirect(offs_sb[:, k * (G // 16) : (k + 1) * (G // 16)]),
@@ -127,31 +132,40 @@ def tile_moe_pre_mlp_relu2_kernel(
                 ALU.mult,
             )
 
+        def woven(tile):
+            return tile[:].rearrange("p (c i t) -> p c t i", i=4, t=PACK)
+
+        def planes(k, c0, c1):
+            return gated[k][:, :, c0:c1].rearrange("p t (c i) -> p c t i", i=4)
+
         def weave(e):
-            k, odd = divmod(e, 2)
-            x_bf[e] = link([P, C * PACK], BF16, ("odd" if odd else "even") + str(k))
-            for c0, c1 in [(0, C)] if odd else [(0, P), (P, C)]:
-                dst = x_bf[e][:, c0 * PACK : c1 * PACK].rearrange("p (c i t) -> p c t i", i=4, t=PACK)
-                src = gated[k][:, :, odd * C + c0 : odd * C + c1].rearrange("p t (c i) -> p c t i", i=4)
-                if odd:
-                    nc.scalar.copy(dst, src)
-                else:
-                    nc.vector.tensor_copy(dst, src)
+            k = e // 2
+            if e % 2:
+                x_bf[e] = [link([P, C * PACK], BF16, "odd" + str(k))]
+                nc.scalar.copy(woven(x_bf[e][0]), planes(k, C, G))
+            else:
+                x_bf[e] = []
+                for half in range(2):
+                    x_bf[e].append(placed([P, P * PACK], BF16, "x" + "ab"[half], k + 1, ROOM - 2048 + half * 1024))
+                    nc.vector.tensor_copy(woven(x_bf[e][half]), planes(k, half * P, (half + 1) * P))
+
+        def quantise(parts, label, bufs):
+            codes = ring.tile([P, C], U32, name=label + "_codes", align_bytes=64, bufs=bufs)
+            scales = ring.tile([P, C], U8, name=label + "_scales", align_bytes=64, bufs=bufs)
+            width = C // len(parts)
+            for j, part in enumerate(parts):
+                cols = slice(j * width, (j + 1) * width)
+                nc.vector.quantize_mx(out=codes[:, cols].bitcast(FP8X4), scales=scales[:, cols], in_=part)
+            return codes, scales
 
         def quantise_x(e):
-            codes = ring.tile([P, C], U32, name="x_codes", align_bytes=64, bufs=4)
-            scales = ring.tile([P, C], U8, name="x_scales", align_bytes=64, bufs=4)
-            for c0, c1 in [(0, C)] if e % 2 else [(0, P), (P, C)]:
-                nc.vector.quantize_mx(
-                    out=codes[:, c0:c1].bitcast(FP8X4), scales=scales[:, c0:c1], in_=x_bf[e][:, c0 * PACK : c1 * PACK]
-                )
-            x_q[e] = codes, scales
+            x_q[e] = quantise([part[:] for part in x_bf[e]], "x", 4)
 
         def quantise_h(e):
-            codes = ring.tile([P, C], U32, name="h_codes", align_bytes=64)
-            scales = ring.tile([P, C], U8, name="h_scales", align_bytes=64)
-            nc.vector.quantize_mx(out=codes[:].bitcast(FP8X4), scales=scales[:], in_=h_bf[e][:])
-            h_q[e] = codes, scales
+            if e == LAST:
+                h_q[e] = quantise([h_bf[e][:, : P * PACK], h_bf[e][:, P * PACK :]], "h", 3)
+            else:
+                h_q[e] = quantise([h_bf[e][:]], "h", 3)
 
         def first_product(e):
             codes, scales = x_q[e]
@@ -177,7 +191,7 @@ def tile_moe_pre_mlp_relu2_kernel(
                     relu.append(ring.tile([P, PACK, P], F32, name="relu", align_bytes=64))
                 dst = relu[half][:].rearrange("p t (c i) -> p c t i", i=2)
                 src = pre[e, half][:].rearrange("p (c i t) -> p c t i", i=2, t=PACK)
-                if e >= E - 2 and half:
+                if e == LAST - 1 or (e == LAST and half):
                     nc.vector.tensor_scalar_max(dst, src, 0.0)
                 else:
                     nc.scalar.activation(dst, src, ACT.Relu)
@@ -190,34 +204,36 @@ def tile_moe_pre_mlp_relu2_kernel(
             if half == 0 and e % 2:
                 h_bf[e] = ring.tile([P, C * PACK], BF16, name="h_odd", align_bytes=64)
             elif half == 0:
-                h_bf[e] = link([P, C * PACK], BF16, "even" + str(e // 2 + 1))
+                h_bf[e] = placed([P, C * PACK], BF16, "h", e // 2 + 2, ROOM - 2048)
             nc.scalar.activation(
                 h_bf[e][:, half * P * PACK : (half + 1) * P * PACK].rearrange("p (s t) -> p s t", t=PACK),
                 turned[e, half][:].rearrange("p t s -> p s t"),
                 ACT.Square,
             )
 
-        def second_product(e):
+        def second_product(e, c0=0, c1=C):
             codes, scales = h_q[e]
             if e % 2 and e < LAST:
                 acc[e] = bank([P, C], e + 1, 0)
-            else:
+            elif e < LAST:
                 acc[e] = psum.tile([P, C], F32, name="acc", bufs=2)
+            else:
+                acc[e] = psum.tile([P, P], F32, name="acc_last", bufs=2)
             nc.tensor.matmul_mx(
                 out=acc[e][:],
                 lhsT=w2_of[e].bitcast(FP4X4),
                 lhsT_scale=s2_of[e],
-                rhs=codes[:].bitcast(FP8X4),
-                rhs_scale=scales[:],
+                rhs=codes[:, c0:c1].bitcast(FP8X4),
+                rhs_scale=scales[:, c0:c1],
                 start=True,
                 stop=True,
             )
 
-        def keep_result(e):
-            if e in (E - 4, E - 3):
-                nc.vector.tensor_copy(y_sb[:, e * C : (e + 1) * C], acc[e][:])
+        def keep_result(e, c0=0, c1=C):
+            if e in (E - 4, E - 3, LAST):
+                nc.vector.tensor_copy(y_sb[:, e * C + c0 : e * C + c1], acc[e][:])
             else:
-                nc.scalar.copy(y_sb[:, e * C : (e + 1) * C], acc[e][:])
+                nc.scalar.copy(y_sb[:, e * C + c0 : e * C + c1], acc[e][:])
 
         for t in range(PACK):
             gather(0, t)
@@ -255,8 +271,9 @@ def tile_moe_pre_mlp_relu2_kernel(
         second_product(LAST - 1)
         quantise_h(LAST)
         keep_result(LAST - 1)
-        second_product(LAST)
-        keep_result(LAST)
+        for half in range(2):
+            second_product(LAST, half * P, (half + 1) * P)
+            keep_result(LAST, half * P, (half + 1) * P)
 
         first = keep.tile([P, T], F32, name="first", align_bytes=64)
         for half in range(2):

@@ -189,8 +189,8 @@ def tile_moe_pre_mlp_relu2_kernel(
                     relu.append(link([P, PACK, P], F32, "odd" + str(e // 2 + 1)))
                 else:
                     relu.append(ring.tile([P, PACK, P], F32, name="relu", align_bytes=64))
-                dst = relu[half][:].rearrange("p t (c i) -> p c t i", i=2)
-                src = pre[e, half][:].rearrange("p (c i t) -> p c t i", i=2, t=PACK)
+                dst = relu[half][:].rearrange("p t (c i) -> p c t i", i=4)
+                src = pre[e, half][:].rearrange("p (c i t) -> p c t i", i=4, t=PACK)
                 if e == LAST - 1 or (e == LAST and half):
                     nc.vector.tensor_scalar_max(dst, src, 0.0)
                 else:

from contextlib import ExitStack

import concourse.mybir as mybir
from concourse.masks import make_identity

K, T, E, C, H, N = 512, 1280, 10, 256, 512, 128
S = E * C
FLOPS = 2 * S * (K * H + H * N)

F32 = mybir.dt.float32
BF16 = mybir.dt.bfloat16
I32 = mybir.dt.int32
U32 = mybir.dt.uint32
U16 = mybir.dt.uint16
U8 = mybir.dt.uint8
FP8X4 = mybir.dt.float8_e4m3fn_x4
FP4X4 = mybir.dt.float4_e2m1fn_x4
ALU = mybir.AluOpType
ACT = mybir.ActivationFunctionType

P = 128
PACK = 4
PAIRS = E // 2
G = 2 * C
LAST = E - 1
GATE_CUTS = (0, 1, 2, 5)
W1_CUTS = (0, 2, 6, 10)
S1_CUTS = (0, 2, 10)
OUT_CUTS = (0, 640, 1088, 1280)
ROOM = 9216


def tile_moe_pre_mlp_relu2_kernel(
    tc, xT, w1_words, w1_scales, w2_words, w2_scales, gate, offs, pos1, pos2, out
):
    nc = tc.nc
    with ExitStack() as ctx:
        lists = ctx.enter_context(tc.tile_pool(name="lists", bufs=1))
        keep = ctx.enter_context(tc.tile_pool(name="keep", bufs=1))
        chain = ctx.enter_context(tc.tile_pool(name="chain", bufs=1))
        arena = ctx.enter_context(tc.tile_pool(name="arena", bufs=1))
        ring = ctx.enter_context(tc.tile_pool(name="ring", bufs=3))
        psum = ctx.enter_context(tc.psum_pool(name="psum", bufs=1))

        offs_sb = lists.tile([P, S // 16], U16, name="offs_sb")
        pos1_sb = lists.tile([P, T // 16], U16, name="pos1_sb")
        pos2_sb = lists.tile([P, T // 16], U16, name="pos2_sb")

        def pieces(cuts, width, dtype, label):
            tiles = []
            where = {}
            for j in range(len(cuts) - 1):
                tile = keep.tile([P, (cuts[j + 1] - cuts[j]) * width], dtype, name=label + str(j), align_bytes=64)
                tiles.append(tile)
                for e in range(cuts[j], cuts[j + 1]):
                    where[e] = tile[:, (e - cuts[j]) * width : (e - cuts[j] + 1) * width]
            return tiles, where

        x_sb = [keep.tile([P, T], F32, name="x" + str(t), align_bytes=64) for t in range(PACK)]
        gate_tiles, gate_of = pieces(GATE_CUTS, G, F32, "gate")
        w1_tiles, w1_of = pieces(W1_CUTS, 2 * H, U8, "w1")
        s1_tiles, s1_of = pieces(S1_CUTS, H, U8, "s1")
        w2_tiles, w2_of = pieces((0, E), 2 * N, U8, "w2")
        s2_tiles, s2_of = pieces((0, E), N, U8, "s2")
        y_sb = keep.tile([P, S], F32, name="y_sb", align_bytes=64)

        nc.gpsimd.memset(s1_tiles[0][:].bitcast(I32), 0)
        for plane in s2_tiles + s1_tiles[1:]:
            nc.vector.memset(plane[:].bitcast(I32), 0)

        made = keep.tile([P, P], F32, name="made")
        ident = keep.tile([P, P], F32, name="ident")
        make_identity(nc, made[:])
        nc.scalar.activation(ident[:], made[:], ACT.Relu)

        x_rows = xT.rearrange("(p t) w -> p t w", t=PACK)

        def load_gate(j):
            nc.sync.dma_start(gate_tiles[j][:], gate[0:P, GATE_CUTS[j] * G : GATE_CUTS[j + 1] * G])

        def load_words(tile, words, e0, e1):
            nc.sync.dma_start(
                tile[:].bitcast(I32).rearrange("p (e n) -> p e n", e=e1 - e0),
                words.rearrange("e s p n -> p (e s) n")[:, e0:e1, :].bitcast(I32),
            )

        def load_scales(tile, scales, e0, e1):
            rows = scales.rearrange("e s (q r) n -> r q (e s) n", r=4)
            for r in range(4):
                nc.sync.dma_start(
                    tile[r:P:32, :].bitcast(I32).rearrange("p (e n) -> p e n", e=e1 - e0),
                    rows[r][:, e0:e1, :].bitcast(I32),
                )

        nc.sync.dma_start(offs_sb[:], offs)
        nc.sync.dma_start(x_sb[0][:], x_rows[:, 0, :])
        load_gate(0)
        for t in range(1, PACK):
            nc.sync.dma_start(x_sb[t][:], x_rows[:, t, :])
        load_words(w1_tiles[0], w1_words, W1_CUTS[0], W1_CUTS[1])
        load_scales(s1_tiles[0], w1_scales, S1_CUTS[0], S1_CUTS[1])
        load_gate(1)
        load_words(w2_tiles[0], w2_words, 0, E)
        load_scales(s2_tiles[0], w2_scales, 0, E)
        load_words(w1_tiles[1], w1_words, W1_CUTS[1], W1_CUTS[2])
        load_scales(s1_tiles[1], w1_scales, S1_CUTS[1], S1_CUTS[2])
        load_gate(2)
        load_words(w1_tiles[2], w1_words, W1_CUTS[2], W1_CUTS[3])
        nc.sync.dma_start(pos1_sb[:], pos1)
        nc.sync.dma_start(pos2_sb[:], pos2)

        gated, x_bf, x_q, pre, turned, h_bf, h_q, acc = {}, {}, {}, {}, {}, {}, {}, {}

        def link(shape, dtype, tag):
            return chain.tile(shape, dtype, name="link", tag=tag, align_bytes=64)

        def placed(shape, dtype, name, k, start):
            return arena.tile(shape, dtype, name=name + str(k), align_bytes=64, offset=k * ROOM + start)

        def bank(shape, e, half):
            return psum.tile(shape, F32, name="bank", tag="bank" + str(e % 2) + str(half))

        def gather(k, t):
            if k == PAIRS:
                return
            if t == 0:
                gated[k] = placed([P, PACK, G], F32, "gated", k, 0)
            nc.vector.tensor_tensor(
                gated[k][:, t, :],
                x_sb[t][:].indirect(offs_sb[:, k * (G // 16) : (k + 1) * (G // 16)]),
                gate_of[k],
                ALU.mult,
            )

        def woven(tile):
            return tile[:].rearrange("p (c i t) -> p c t i", i=4, t=PACK)

        def planes(k, c0, c1):
            return gated[k][:, :, c0:c1].rearrange("p t (c i) -> p c t i", i=4)

        def weave(e):
            k = e // 2
            if e % 2:
                x_bf[e] = [link([P, C * PACK], BF16, "odd" + str(k))]
                nc.scalar.copy(woven(x_bf[e][0]), planes(k, C, G))
            else:
                x_bf[e] = []
                for half in range(2):
                    x_bf[e].append(placed([P, P * PACK], BF16, "x" + "ab"[half], k + 1, ROOM - 2048 + half * 1024))
                    nc.vector.tensor_copy(woven(x_bf[e][half]), planes(k, half * P, (half + 1) * P))

        def quantise(parts, label, bufs):
            codes = ring.tile([P, C], U32, name=label + "_codes", align_bytes=64, bufs=bufs)
            scales = ring.tile([P, C], U8, name=label + "_scales", align_bytes=64, bufs=bufs)
            width = C // len(parts)
            for j, part in enumerate(parts):
                cols = slice(j * width, (j + 1) * width)
                nc.vector.quantize_mx(out=codes[:, cols].bitcast(FP8X4), scales=scales[:, cols], in_=part)
            return codes, scales

        def quantise_x(e):
            x_q[e] = quantise([part[:] for part in x_bf[e]], "x", 4)

        def quantise_h(e):
            if e == LAST:
                h_q[e] = quantise([h_bf[e][:, : P * PACK], h_bf[e][:, P * PACK :]], "h", 3)
            else:
                h_q[e] = quantise([h_bf[e][:]], "h", 3)

        def first_product(e):
            codes, scales = x_q[e]
            for half in range(2):
                cols = slice(half * P, (half + 1) * P)
                pre[e, half] = bank([P, H], e, half)
                nc.tensor.matmul_mx(
                    out=pre[e, half][:],
                    lhsT=codes[:, cols].bitcast(FP8X4),
                    lhsT_scale=scales[:, cols],
                    rhs=w1_of[e].bitcast(FP4X4),
                    rhs_scale=s1_of[e],
                    start=True,
                    stop=True,
                )

        def relu_and_turn(e):
            relu = []
            for half in range(2):
                if e % 2 and half:
                    relu.append(link([P, PACK, P], F32, "odd" + str(e // 2 + 1)))
                else:
                    relu.append(ring.tile([P, PACK, P], F32, name="relu", align_bytes=64))
                dst = relu[half][:].rearrange("p t (c i) -> p c t i", i=4)
                src = pre[e, half][:].rearrange("p (c i t) -> p c t i", i=4, t=PACK)
                if e == LAST - 1 or (e == LAST and half):
                    nc.vector.tensor_scalar_max(dst, src, 0.0)
                else:
                    nc.scalar.activation(dst, src, ACT.Relu)
            for half in range(2):
                turned[e, half] = bank([P, PACK, P], e, half)
                for t in range(PACK):
                    nc.tensor.transpose(turned[e, half][:, t, :], relu[half][:, t, :], ident[:])

        def square(e, half):
            if half == 0 and e % 2:
                h_bf[e] = ring.tile([P, C * PACK], BF16, name="h_odd", align_bytes=64)
            elif half == 0:
                h_bf[e] = placed([P, C * PACK], BF16, "h", e // 2 + 2, ROOM - 2048)
            nc.scalar.activation(
                h_bf[e][:, half * P * PACK : (half + 1) * P * PACK].rearrange("p (s t) -> p s t", t=PACK),
                turned[e, half][:].rearrange("p t s -> p s t"),
                ACT.Square,
            )

        def second_product(e, c0=0, c1=C):
            codes, scales = h_q[e]
            if e % 2 and e < LAST:
                acc[e] = bank([P, C], e + 1, 0)
            elif e < LAST:
                acc[e] = psum.tile([P, C], F32, name="acc", bufs=2)
            else:
                acc[e] = psum.tile([P, P], F32, name="acc_last", bufs=2)
            nc.tensor.matmul_mx(
                out=acc[e][:],
                lhsT=w2_of[e].bitcast(FP4X4),
                lhsT_scale=s2_of[e],
                rhs=codes[:, c0:c1].bitcast(FP8X4),
                rhs_scale=scales[:, c0:c1],
                start=True,
                stop=True,
            )

        def keep_result(e, c0=0, c1=C):
            if e in (E - 4, E - 3, LAST):
                nc.vector.tensor_copy(y_sb[:, e * C + c0 : e * C + c1], acc[e][:])
            else:
                nc.scalar.copy(y_sb[:, e * C + c0 : e * C + c1], acc[e][:])

        for t in range(PACK):
            gather(0, t)
        for k in range(PAIRS):
            a, b = 2 * k, 2 * k + 1
            if k:
                quantise_h(a - 2)
                second_product(a - 2)
            weave(a)
            weave(b)
            if k:
                square(b - 2, 0)
                square(b - 2, 1)
            quantise_x(a)
            quantise_x(b)
            first_product(a)
            first_product(b)
            gather(k + 1, 0)
            if k:
                quantise_h(b - 2)
                keep_result(a - 2)
            for t in range(1, PACK):
                gather(k + 1, t)
            relu_and_turn(a)
            relu_and_turn(b)
            square(a, 0)
            if k:
                second_product(b - 2)
            square(a, 1)
            if k:
                keep_result(b - 2)
        square(LAST, 0)
        quantise_h(LAST - 1)
        square(LAST, 1)
        second_product(LAST - 1)
        quantise_h(LAST)
        keep_result(LAST - 1)
        for half in range(2):
            second_product(LAST, half * P, (half + 1) * P)
            keep_result(LAST, half * P, (half + 1) * P)

        first = keep.tile([P, T], F32, name="first", align_bytes=64)
        for half in range(2):
            c0, c1 = half * T // 2, (half + 1) * T // 2
            nc.vector.tensor_copy(first[:, c0:c1], y_sb[:].indirect(pos1_sb[:, c0 // 16 : c1 // 16]))
        for j in range(len(OUT_CUTS) - 1):
            c0, c1 = OUT_CUTS[j], OUT_CUTS[j + 1]
            total = keep.tile([P, c1 - c0], F32, name="total" + str(j), align_bytes=64)
            nc.vector.tensor_tensor(
                total[:], y_sb[:].indirect(pos2_sb[:, c0 // 16 : c1 // 16]), first[:, c0:c1], ALU.add
            )
            queue = nc.sync if j % 2 == 0 else nc.scalar
            queue.dma_start(out[:, c0:c1], total[:])
